import numpy as np
import ml_dtypes


def mxq(x, axis, fmt="e4m3"):
    dtype, down = {"e4m3": (ml_dtypes.float8_e4m3fn, 7), "e5m2": (ml_dtypes.float8_e5m2, 14)}[fmt]
    v = np.moveaxis(np.asarray(x, np.float32).astype(ml_dtypes.bfloat16).astype(np.float64), axis, -1)
    blocks = v.reshape(v.shape[:-1] + (-1, 32))
    amax = np.abs(blocks).max(-1, keepdims=True)
    byte = np.maximum(np.where(amax > 0, np.frexp(amax)[1] - 1 + 127, 0) - down, 1)
    scale = np.exp2(byte - 127.0)
    codes = (blocks / scale).astype(np.float32).astype(dtype).astype(np.float64)
    return np.moveaxis((codes * scale).reshape(v.shape), -1, axis)


WIDE = False


def mx_kscale(k, group=512):
    if not WIDE:
        return np.ones(k)
    levels = np.array([10, -10, 5, -5, 0])
    if group != 512:
        return np.exp2(np.random.permutation(np.resize(levels, k // group))).repeat(group)
    if k % 512:
        return np.exp2(np.random.permutation(np.resize(levels, k // 32))).repeat(32)
    a = np.empty((k // 512, 16))
    for p in range(k // 512):
        a[p, :8] = np.random.permutation(np.resize(levels, 8))
        for g in range(8):
            far = levels[np.abs(levels - a[p, g]) >= 10]
            a[p, g + 8] = far[np.random.randint(len(far))]
    return np.exp2(a.ravel()).repeat(32)


def f64(x):
    return np.asarray(x).astype(np.float64)


def striped(idx):
    return np.tile(np.asarray(idx).reshape(-1, 16).T, (8, 1)).astype(np.uint16)


def unstriped(offs):
    return offs[:16].T.reshape(-1).astype(np.int64)


H, KV, D, NQ, N = 4, 4, 128, 512, 1024


def setup_inputs():
    n = np.random.standard_normal
    s = mx_kscale(D, 0)[:, None]
    u = mx_kscale(N)
    t = np.random.uniform(0.5, 2.0, N) * u
    v = n((KV, N, 128))
    return {
        "qT": (n((H, D, NQ)) * s * (0.70 / np.sqrt(D))).astype(np.float32),
        "kT": (n((KV, D, N)) / s).astype(np.float32),
        "t": t.reshape(N, 1).astype(np.float32),
        "v": (v / t[:, None]).astype(np.float32),
        "og": n((H, NQ, 128)).astype(np.float32),
    }


def reference(qT, kT, t, v, og):
    a = mxq(f64(kT), 1, "e4m3").transpose(0, 2, 1) @ mxq(f64(qT), 1, "e4m3")
    p = np.tanh(a)
    w = p * f64(t)
    y = mxq(w, 1, "e4m3").transpose(0, 2, 1) @ mxq(f64(v), 1, "e4m3")
    y = y / 16.0
    y = y / (1.0 + np.exp(-f64(og)))
    return y

@@ -1,0 +1,292 @@
+from contextlib import ExitStack
+
+import concourse.mybir as mybir
+
+H, D, NQ, N, E = 4, 128, 512, 1024, 128
+FLOPS = 2 * H * N * NQ * (D + E)
+
+F32 = mybir.dt.float32
+BF16 = mybir.dt.bfloat16
+U32 = mybir.dt.uint32
+U8 = mybir.dt.uint8
+FP8X4 = mybir.dt.float8_e4m3fn_x4
+ACT = mybir.ActivationFunctionType
+ALU = mybir.AluOpType
+
+P = 128
+PACK = 4
+ROWS = D // PACK
+PASS = P * PACK
+PASSES = N // PASS
+QT = 128
+QTILES = NQ // QT
+STEPS = PASSES * QTILES
+CHUNK = 256
+CS = CHUNK // PACK
+LINE = 4
+HEAD_V_SHARE = 40
+
+
+def tile_rows_a_tanh_gate_kernel(tc, qT, kT, t, v, og, out):
+    nc = tc.nc
+    q_hbm = qT.rearrange("h (p j) n -> (h p) j n", j=PACK)
+    k_hbm = kT.rearrange("h (p j) n -> (h p) j n", j=PACK)
+    v_hbm = v.rearrange("h (g p j) e -> g p h (j e)", p=P, j=PACK)
+    og_hbm = og.rearrange("h (c q) e -> c q h e", q=QT)
+    out_hbm = out.rearrange("h (c q) e -> c q h e", q=QT)
+    t_hbm = t.rearrange("(g p j) o -> p g (j o)", p=P, j=PACK)
+
+    with ExitStack() as ctx:
+        keep = ctx.enter_context(tc.tile_pool(name="keep", bufs=1))
+        ring = ctx.enter_context(tc.tile_pool(name="ring", bufs=3))
+        psum = ctx.enter_context(tc.psum_pool(name="psum", bufs=1))
+        ctx.enter_context(tc.manual_schedule())
+
+        def sb(name, shape, dtype):
+            return keep.tile(shape, dtype, name=name, align_bytes=64)
+
+        t_sb = sb("t_sb", [P, PASSES, PACK], F32)
+        warm = sb("warm", [P, 8], F32)
+        warm_out = sb("warm_out", [P, 8], F32)
+        q_raw = [sb("q_raw0", [P, PACK, QT], F32), sb("q_raw1", [P, PACK, QT], F32), sb("q_raw23", [P, PACK, 2 * QT], F32)]
+        k_raw = [sb("k_raw%d" % c, [P, PACK, CHUNK], F32) for c in range(N // CHUNK)]
+        v_raw = [sb("v_raw%d" % g, [P, H, PACK * E], F32) for g in range(PASSES)]
+        og_raw = [sb("og_raw%d" % c, [P, H, E], F32) for c in range(QTILES)]
+        q_bf = sb("q_bf", [P, NQ, PACK], BF16)
+        k_bf = [sb("k_bf%d" % g, [P, PACK, P, PACK], BF16) for g in range(PASSES)]
+        v_bf = [sb("v_bf%d" % g, [P, H, E, PACK], BF16) for g in range(PASSES)]
+        q_codes = sb("q_codes", [P, NQ], U32)
+        q_scales = sb("q_scales", [P, NQ], U8)
+        k_codes = [sb("k_codes%d" % g, [P, PASS], U32) for g in range(PASSES)]
+        k_scales = [sb("k_scales%d" % g, [P, PASS], U8) for g in range(PASSES)]
+        v_codes = [sb("v_codes%d" % g, [P, H * E], U32) for g in range(PASSES)]
+        v_scales = [sb("v_scales%d" % g, [P, H * E], U8) for g in range(PASSES)]
+        w_codes = [sb("w_codes%d" % s, [P, H * QT], U32) for s in range(STEPS)]
+        w_scales = [sb("w_scales%d" % s, [P, H * QT], U8) for s in range(STEPS)]
+        gate = [sb("gate%d" % c, [P, H, E], F32) for c in range(QTILES)]
+        res = [sb("res%d" % c, [P, H, E], F32) for c in range(QTILES)]
+        score_ps = [psum.tile([P, PACK, QT], F32, name="score_ps%d" % h) for h in range(H)]
+        y_ps = [psum.tile([P, H, E], F32, name="y_ps%d" % c) for c in range(QTILES)]
+        p_sb = {}
+        w_bf = {}
+
+        def copy_on(engine, dst, src):
+            if engine == "vector":
+                nc.vector.tensor_copy(out=dst, in_=src)
+            else:
+                nc.scalar.copy(out=dst, in_=src)
+
+        def quantize(codes, scales, src):
+            nc.vector.quantize_mx(out=codes.bitcast(FP8X4), scales=scales, in_=src)
+
+        def q_source(c):
+            return q_raw[c][:] if c < 2 else q_raw[2][:, :, (c - 2) * QT : (c - 1) * QT]
+
+        def cast_q(c):
+            nc.vector.tensor_copy(
+                out=q_bf[:, c * QT : (c + 1) * QT, :].rearrange("p (c i) j -> p c j i", i=LINE),
+                in_=q_source(c).rearrange("p j (c i) -> p c j i", i=LINE),
+            )
+
+        def quantize_q(c0, c1):
+            cols = slice(c0 * QT, c1 * QT)
+            quantize(q_codes[:, cols], q_scales[:, cols], q_bf[:, cols, :].rearrange("p n j -> p (n j)"))
+
+        def cast_k(engine, c, s0, s1):
+            g, first = divmod(c * CS, P)
+            copy_on(
+                engine,
+                k_bf[g][:, :, first + s0 : first + s1, :].rearrange("p r s j -> p s j r"),
+                k_raw[c][:, :, s0 * PACK : s1 * PACK].rearrange("p j (s r) -> p s j r", r=PACK),
+            )
+
+        def quantize_k_part(c, r):
+            g, first = divmod(c * CS, P)
+            cols = slice(r * P + first, r * P + first + CS)
+            quantize(
+                k_codes[g][:, cols],
+                k_scales[g][:, cols],
+                k_bf[g][:, r, first : first + CS, :].rearrange("p s j -> p (s j)"),
+            )
+
+        def quantize_k(g):
+            quantize(k_codes[g][:], k_scales[g][:], k_bf[g][:].rearrange("p r s j -> p (r s j)"))
+
+        def cast_v(g, h):
+            nc.scalar.copy(
+                out=v_bf[g][:, h, :, :].rearrange("p (c i) j -> p c j i", i=LINE),
+                in_=v_raw[g][:, h, :].rearrange("p (j c i) -> p c j i", j=PACK, i=LINE),
+            )
+
+        def quantize_v(g):
+            quantize(v_codes[g][:], v_scales[g][:], v_bf[g][:].rearrange("p h e j -> p (h e j)"))
+
+        def score(s, h, r):
+            g, c = divmod(s, QTILES)
+            rows = slice(h * ROWS, (h + 1) * ROWS)
+            tok = slice(r * P, (r + 1) * P)
+            qs = slice(c * QT, (c + 1) * QT)
+            nc.tensor.matmul_mx(
+                out=score_ps[h][:, r, :],
+                lhsT=k_codes[g][rows, tok].bitcast(FP8X4),
+                lhsT_scale=k_scales[g][rows, tok],
+                rhs=q_codes[rows, qs].bitcast(FP8X4),
+                rhs_scale=q_scales[rows, qs],
+                start=True,
+                stop=True,
+            )
+
+        def tanh(s, h):
+            if h == 0:
+                p_sb[s] = ring.tile([P, H, QT, PACK], F32, name="p_sb")
+            nc.scalar.activation(
+                out=p_sb[s][:, h, :, :], in_=score_ps[h][:].rearrange("p r q -> p q r"), func=ACT.Tanh
+            )
+            if s + 1 < STEPS:
+                for r in range(PACK):
+                    score(s + 1, h, r)
+
+        def weigh(s, h0, h1):
+            if h0 == 0:
+                w_bf[s] = ring.tile([P, H, QT, PACK], BF16, name="w_bf", align_bytes=64)
+            n = (h1 - h0) * QT
+            nc.vector.tensor_tensor(
+                out=w_bf[s][:, h0:h1, :, :].rearrange("p h q r -> p (h q) r"),
+                in0=p_sb[s][:, h0:h1, :, :].rearrange("p h q r -> p (h q) r"),
+                in1=t_sb[:, s // QTILES, :].unsqueeze(1).to_broadcast([P, n, PACK]),
+                op=ALU.mult,
+            )
+
+        def quantize_w(s, h0, h1):
+            cols = slice(h0 * QT, h1 * QT)
+            quantize(
+                w_codes[s][:, cols], w_scales[s][:, cols], w_bf[s][:, h0:h1, :, :].rearrange("p h q r -> p (h q r)")
+            )
+
+        def y_bank(c, h):
+            return y_ps[0] if (c == QTILES - 1 and h >= 2) else y_ps[c]
+
+        def mix(c, h0, h1):
+            for h in range(h0, h1):
+                cols = slice(h * QT, (h + 1) * QT)
+                for g in range(PASSES):
+                    s = g * QTILES + c
+                    nc.tensor.matmul_mx(
+                        out=y_bank(c, h)[:, h, :],
+                        lhsT=w_codes[s][:, cols].bitcast(FP8X4),
+                        lhsT_scale=w_scales[s][:, cols],
+                        rhs=v_codes[g][:, cols].bitcast(FP8X4),
+                        rhs_scale=v_scales[g][:, cols],
+                        start=(g == 0),
+                        stop=(g == PASSES - 1),
+                    )
+
+        def sigmoid(c):
+            nc.scalar.activation(out=gate[c][:], in_=og_raw[c][:], func=ACT.Sigmoid)
+
+        def finish(c, h0, h1):
+            nc.vector.scalar_tensor_tensor(
+                out=res[c][:, h0:h1, :].rearrange("p h e -> p (h e)"),
+                in0=y_bank(c, h0)[:, h0:h1, :].rearrange("p h e -> p (h e)"),
+                scalar=1.0 / 16.0,
+                in1=gate[c][:, h0:h1, :].rearrange("p h e -> p (h e)"),
+                op0=ALU.mult,
+                op1=ALU.mult,
+            )
+            nc.sync.dma_start(out=out_hbm[c][:, h0:h1, :], in_=res[c][:, h0:h1, :])
+
+        nc.sync.dma_start(out=q_raw[0][:], in_=q_hbm[:, :, 0:QT])
+        for c in range(2):
+            nc.sync.dma_start(out=k_raw[c][:], in_=k_hbm[:, :, c * CHUNK : (c + 1) * CHUNK])
+        nc.sync.dma_start(out=t_sb[:], in_=t_hbm)
+        nc.sync.dma_start(out=q_raw[1][:], in_=q_hbm[:, :, QT : 2 * QT])
+        nc.sync.dma_start(out=q_raw[2][:], in_=q_hbm[:, :, 2 * QT : 4 * QT])
+        for c in range(2, 4):
+            nc.sync.dma_start(out=k_raw[c][:], in_=k_hbm[:, :, c * CHUNK : (c + 1) * CHUNK])
+        for g in range(PASSES):
+            for h0 in range(0, H, 2):
+                nc.sync.dma_start(out=v_raw[g][:, h0 : h0 + 2, :], in_=v_hbm[g][:, h0 : h0 + 2, :])
+        for c in range(QTILES):
+            nc.sync.dma_start(out=og_raw[c][:], in_=og_hbm[c])
+
+        nc.vector.memset(warm[:], 0.0)
+        nc.scalar.activation(out=warm_out[:], in_=warm[:], func=ACT.Sigmoid)
+
+        cast_q(0)
+        cast_k("scalar", 0, HEAD_V_SHARE, CS)
+        cast_k("vector", 0, 0, HEAD_V_SHARE)
+        quantize_q(0, 1)
+        quantize_k_part(0, 0)
+        quantize_k_part(0, 1)
+        cast_k("scalar", 1, HEAD_V_SHARE, CS)
+        cast_k("vector", 1, 0, HEAD_V_SHARE)
+        quantize_k_part(0, 2)
+        quantize_k_part(0, 3)
+        for r in range(PACK):
+            quantize_k_part(1, r)
+            for h in range(H):
+                score(0, h, r)
+        cast_q(1)
+        cast_q(2)
+        quantize_q(1, 2)
+
+        half = CS // 2
+        scalar_casts = [lambda: cast_k("scalar", 2, 0, half), lambda: cast_k("scalar", 2, half, CS)]
+        scalar_casts += [(lambda g=g, h=h: cast_v(g, h)) for g in range(PASSES) for h in range(H)]
+        cast_slots = [(0, 3), (1, 1), (1, 3), (2, 1), (2, 3), (3, 1), (3, 3), (4, 3), (5, 3), (5, 3)]
+        scalar_extra = {}
+        for slot, job in zip(cast_slots, scalar_casts):
+            scalar_extra.setdefault(slot, []).append(job)
+        scalar_extra[(6, 1)] = [lambda: mix(0, 0, H)]
+        scalar_extra[(6, 3)] = [lambda: sigmoid(0), lambda: mix(1, 0, H)]
+        vector_extra = {
+            (0, 0): [lambda: cast_q(3)],
+            (0, 1): [lambda: quantize_q(2, 4)],
+            (1, 0): [lambda: cast_k("vector", 3, 0, CS)],
+            (2, 0): [lambda: quantize_k(1)],
+            (3, 0): [lambda: quantize_v(0)],
+            (5, 1): [lambda: quantize_v(1)],
+            (6, 1): [lambda: finish(0, 0, H)],
+        }
+
+        last = STEPS - 1
+        pending = None
+        for s in range(last):
+            for pair in range(2):
+                h0 = 2 * pair
+                for h in (h0, h0 + 1):
+                    tanh(s, h)
+                    if s == 0:
+                        weigh(s, h, h + 1)
+                    for job in scalar_extra.get((s, h), []):
+                        job()
+                if s > 0:
+                    weigh(s, h0, h0 + 2)
+                if pending is not None:
+                    quantize_w(*pending)
+                pending = (s, h0, h0 + 2)
+                for job in vector_extra.get((s, pair), []):
+                    job()
+
+        tanh(last, 0)
+        tanh(last, 1)
+        sigmoid(1)
+        weigh(last, 0, 2)
+        quantize_w(*pending)
+        mix(2, 0, H)
+        finish(1, 0, H)
+        tanh(last, 2)
+        sigmoid(2)
+        weigh(last, 2, 3)
+        quantize_w(last, 0, 2)
+        mix(3, 0, 2)
+        finish(2, 0, H)
+        tanh(last, 3)
+        sigmoid(3)
+        weigh(last, 3, 4)
+        quantize_w(last, 2, 3)
+        mix(3, 2, 3)
+        finish(3, 0, 2)
+        quantize_w(last, 3, 4)
+        mix(3, 3, 4)
+        finish(3, 2, 4)

@@ -34,7 +34,7 @@ def tile_rows_a_tanh_gate_kernel(tc, qT, kT, t, v, og, out):
     v_hbm = v.rearrange("h (g p j) e -> g p h (j e)", p=P, j=PACK)
     og_hbm = og.rearrange("h (c q) e -> c q h e", q=QT)
     out_hbm = out.rearrange("h (c q) e -> c q h e", q=QT)
-    t_hbm = t.rearrange("(g p j) o -> p g (j o)", p=P, j=PACK)
+    t_hbm = t.rearrange("(g p j) o -> g p (j o)", p=P, j=PACK)
 
     with ExitStack() as ctx:
         keep = ctx.enter_context(tc.tile_pool(name="keep", bufs=1))
@@ -45,10 +45,11 @@ def tile_rows_a_tanh_gate_kernel(tc, qT, kT, t, v, og, out):
         def sb(name, shape, dtype):
             return keep.tile(shape, dtype, name=name, align_bytes=64)
 
-        t_sb = sb("t_sb", [P, PASSES, PACK], F32)
+        t_sb = [sb("t_sb%d" % g, [P, PACK], F32) for g in range(PASSES)]
         warm = sb("warm", [P, 8], F32)
         warm_out = sb("warm_out", [P, 8], F32)
-        q_raw = [sb("q_raw0", [P, PACK, QT], F32), sb("q_raw1", [P, PACK, QT], F32), sb("q_raw23", [P, PACK, 2 * QT], F32)]
+        q_loads = [(0, 1), (1, 2), (2, 4)]
+        q_raw = [sb("q_raw%d" % c0, [P, PACK, (c1 - c0) * QT], F32) for c0, c1 in q_loads]
         k_raw = [sb("k_raw%d" % c, [P, PACK, CHUNK], F32) for c in range(N // CHUNK)]
         v_raw = [sb("v_raw%d" % g, [P, H, PACK * E], F32) for g in range(PASSES)]
         og_raw = [sb("og_raw%d" % c, [P, H, E], F32) for c in range(QTILES)]
@@ -79,13 +80,16 @@ def tile_rows_a_tanh_gate_kernel(tc, qT, kT, t, v, og, out):
         def quantize(codes, scales, src):
             nc.vector.quantize_mx(out=codes.bitcast(FP8X4), scales=scales, in_=src)
 
-        def q_source(c):
-            return q_raw[c][:] if c < 2 else q_raw[2][:, :, (c - 2) * QT : (c - 1) * QT]
+        def load_q(part):
+            c0, c1 = q_loads[part]
+            nc.sync.dma_start(out=q_raw[part][:], in_=q_hbm[:, :, c0 * QT : c1 * QT])
 
-        def cast_q(c):
-            nc.vector.tensor_copy(
-                out=q_bf[:, c * QT : (c + 1) * QT, :].rearrange("p (c i) j -> p c j i", i=LINE),
-                in_=q_source(c).rearrange("p j (c i) -> p c j i", i=LINE),
+        def cast_q(engine, part):
+            c0, c1 = q_loads[part]
+            copy_on(
+                engine,
+                q_bf[:, c0 * QT : c1 * QT, :].rearrange("p (c i) j -> p c j i", i=LINE),
+                q_raw[part][:].rearrange("p j (c i) -> p c j i", i=LINE),
             )
 
         def quantize_q(c0, c1):
@@ -112,10 +116,11 @@ def tile_rows_a_tanh_gate_kernel(tc, qT, kT, t, v, og, out):
         def quantize_k(g):
             quantize(k_codes[g][:], k_scales[g][:], k_bf[g][:].rearrange("p r s j -> p (r s j)"))
 
-        def cast_v(g, h):
-            nc.scalar.copy(
-                out=v_bf[g][:, h, :, :].rearrange("p (c i) j -> p c j i", i=LINE),
-                in_=v_raw[g][:, h, :].rearrange("p (j c i) -> p c j i", j=PACK, i=LINE),
+        def cast_v(engine, g, h):
+            copy_on(
+                engine,
+                v_bf[g][:, h, :, :].rearrange("p (c i) j -> p c j i", i=LINE),
+                v_raw[g][:, h, :].rearrange("p (j c i) -> p c j i", j=PACK, i=LINE),
             )
 
         def quantize_v(g):
@@ -138,7 +143,7 @@ def tile_rows_a_tanh_gate_kernel(tc, qT, kT, t, v, og, out):
 
         def tanh(s, h):
             if h == 0:
-                p_sb[s] = ring.tile([P, H, QT, PACK], F32, name="p_sb")
+                p_sb[s] = ring.tile([P, H, QT, PACK], F32, name="p_sb", bufs=4)
             nc.scalar.activation(
                 out=p_sb[s][:, h, :, :], in_=score_ps[h][:].rearrange("p r q -> p q r"), func=ACT.Tanh
             )
@@ -153,7 +158,7 @@ def tile_rows_a_tanh_gate_kernel(tc, qT, kT, t, v, og, out):
             nc.vector.tensor_tensor(
                 out=w_bf[s][:, h0:h1, :, :].rearrange("p h q r -> p (h q) r"),
                 in0=p_sb[s][:, h0:h1, :, :].rearrange("p h q r -> p (h q) r"),
-                in1=t_sb[:, s // QTILES, :].unsqueeze(1).to_broadcast([P, n, PACK]),
+                in1=t_sb[s // QTILES][:].unsqueeze(1).to_broadcast([P, n, PACK]),
                 op=ALU.mult,
             )
 
@@ -166,10 +171,10 @@ def tile_rows_a_tanh_gate_kernel(tc, qT, kT, t, v, og, out):
         def y_bank(c, h):
             return y_ps[0] if (c == QTILES - 1 and h >= 2) else y_ps[c]
 
-        def mix(c, h0, h1):
+        def mix(c, h0, h1, passes=range(PASSES)):
             for h in range(h0, h1):
                 cols = slice(h * QT, (h + 1) * QT)
-                for g in range(PASSES):
+                for g in passes:
                     s = g * QTILES + c
                     nc.tensor.matmul_mx(
                         out=y_bank(c, h)[:, h, :],
@@ -184,7 +189,7 @@ def tile_rows_a_tanh_gate_kernel(tc, qT, kT, t, v, og, out):
         def sigmoid(c):
             nc.scalar.activation(out=gate[c][:], in_=og_raw[c][:], func=ACT.Sigmoid)
 
-        def finish(c, h0, h1):
+        def finish(c, h0, h1, queue):
             nc.vector.scalar_tensor_tensor(
                 out=res[c][:, h0:h1, :].rearrange("p h e -> p (h e)"),
                 in0=y_bank(c, h0)[:, h0:h1, :].rearrange("p h e -> p (h e)"),
@@ -193,16 +198,17 @@ def tile_rows_a_tanh_gate_kernel(tc, qT, kT, t, v, og, out):
                 op0=ALU.mult,
                 op1=ALU.mult,
             )
-            nc.sync.dma_start(out=out_hbm[c][:, h0:h1, :], in_=res[c][:, h0:h1, :])
+            queue.dma_start(out=out_hbm[c][:, h0:h1, :], in_=res[c][:, h0:h1, :])
 
-        nc.sync.dma_start(out=q_raw[0][:], in_=q_hbm[:, :, 0:QT])
+        load_q(0)
         for c in range(2):
             nc.sync.dma_start(out=k_raw[c][:], in_=k_hbm[:, :, c * CHUNK : (c + 1) * CHUNK])
-        nc.sync.dma_start(out=t_sb[:], in_=t_hbm)
-        nc.sync.dma_start(out=q_raw[1][:], in_=q_hbm[:, :, QT : 2 * QT])
-        nc.sync.dma_start(out=q_raw[2][:], in_=q_hbm[:, :, 2 * QT : 4 * QT])
+        load_q(1)
+        load_q(2)
+        nc.sync.dma_start(out=t_sb[0][:], in_=t_hbm[0])
         for c in range(2, 4):
             nc.sync.dma_start(out=k_raw[c][:], in_=k_hbm[:, :, c * CHUNK : (c + 1) * CHUNK])
+        nc.sync.dma_start(out=t_sb[1][:], in_=t_hbm[1])
         for g in range(PASSES):
             for h0 in range(0, H, 2):
                 nc.sync.dma_start(out=v_raw[g][:, h0 : h0 + 2, :], in_=v_hbm[g][:, h0 : h0 + 2, :])
@@ -212,7 +218,7 @@ def tile_rows_a_tanh_gate_kernel(tc, qT, kT, t, v, og, out):
         nc.vector.memset(warm[:], 0.0)
         nc.scalar.activation(out=warm_out[:], in_=warm[:], func=ACT.Sigmoid)
 
-        cast_q(0)
+        cast_q("vector", 0)
         cast_k("scalar", 0, HEAD_V_SHARE, CS)
         cast_k("vector", 0, 0, HEAD_V_SHARE)
         quantize_q(0, 1)
@@ -226,67 +232,64 @@ def tile_rows_a_tanh_gate_kernel(tc, qT, kT, t, v, og, out):
             quantize_k_part(1, r)
             for h in range(H):
                 score(0, h, r)
-        cast_q(1)
-        cast_q(2)
+        cast_q("scalar", 1)
         quantize_q(1, 2)
+        cast_q("vector", 2)
 
-        half = CS // 2
-        scalar_casts = [lambda: cast_k("scalar", 2, 0, half), lambda: cast_k("scalar", 2, half, CS)]
-        scalar_casts += [(lambda g=g, h=h: cast_v(g, h)) for g in range(PASSES) for h in range(H)]
-        cast_slots = [(0, 3), (1, 1), (1, 3), (2, 1), (2, 3), (3, 1), (3, 3), (4, 3), (5, 3), (5, 3)]
-        scalar_extra = {}
-        for slot, job in zip(cast_slots, scalar_casts):
-            scalar_extra.setdefault(slot, []).append(job)
-        scalar_extra[(6, 1)] = [lambda: mix(0, 0, H)]
-        scalar_extra[(6, 3)] = [lambda: sigmoid(0), lambda: mix(1, 0, H)]
-        vector_extra = {
-            (0, 0): [lambda: cast_q(3)],
-            (0, 1): [lambda: quantize_q(2, 4)],
-            (1, 0): [lambda: cast_k("vector", 3, 0, CS)],
-            (2, 0): [lambda: quantize_k(1)],
-            (3, 0): [lambda: quantize_v(0)],
-            (5, 1): [lambda: quantize_v(1)],
-            (6, 1): [lambda: finish(0, 0, H)],
+        scalar_v_slots = [11, 15, 19, 21, 23, 25]
+        after_tanh = {}
+        for i, u in enumerate(scalar_v_slots):
+            after_tanh[u] = [lambda i=i: cast_v("scalar", *divmod(i + 2, H))]
+        after_tanh[27] = [lambda: mix(0, 0, H)]
+        after_weigh = {
+            0: lambda: quantize_q(2, 4),
+            2: lambda: cast_k("vector", 2, 0, CS),
+            5: lambda: cast_k("vector", 3, 0, CS),
+            7: lambda: quantize_k(1),
+            11: lambda: cast_v("vector", 0, 0),
+            13: lambda: cast_v("vector", 0, 1),
+            19: lambda: quantize_v(0),
+            25: lambda: quantize_v(1),
         }
 
         last = STEPS - 1
-        pending = None
         for s in range(last):
-            for pair in range(2):
-                h0 = 2 * pair
-                for h in (h0, h0 + 1):
-                    tanh(s, h)
-                    if s == 0:
-                        weigh(s, h, h + 1)
-                    for job in scalar_extra.get((s, h), []):
-                        job()
-                if s > 0:
-                    weigh(s, h0, h0 + 2)
-                if pending is not None:
-                    quantize_w(*pending)
-                pending = (s, h0, h0 + 2)
-                for job in vector_extra.get((s, pair), []):
+            for h in range(H):
+                u = s * H + h
+                tanh(s, h)
+                for job in after_tanh.get(u, []):
                     job()
+                if s == 0:
+                    weigh(s, h, h + 1)
+                elif h % 2 == 1:
+                    weigh(s, h - 1, h + 1)
+                if s > 0 and h == 1:
+                    quantize_w(s - 1, 0, H)
+                if u in after_weigh:
+                    after_weigh[u]()
 
         tanh(last, 0)
+        mix(1, 0, H)
         tanh(last, 1)
+        sigmoid(0)
         sigmoid(1)
         weigh(last, 0, 2)
-        quantize_w(*pending)
+        quantize_w(last - 1, 0, H)
         mix(2, 0, H)
-        finish(1, 0, H)
+        finish(0, 0, H, nc.sync)
         tanh(last, 2)
         sigmoid(2)
         weigh(last, 2, 3)
         quantize_w(last, 0, 2)
         mix(3, 0, 2)
-        finish(2, 0, H)
+        finish(1, 0, H, nc.sync)
+        finish(2, 0, H, nc.sync)
         tanh(last, 3)
         sigmoid(3)
         weigh(last, 3, 4)
         quantize_w(last, 2, 3)
         mix(3, 2, 3)
-        finish(3, 0, 2)
         quantize_w(last, 3, 4)
         mix(3, 3, 4)
-        finish(3, 2, 4)
+        finish(3, 0, 2, nc.sync)
+        finish(3, 2, 4, nc.scalar)

@@ -21,165 +21,169 @@ PASSES = N // PASS
 QT = 128
 QTILES = NQ // QT
 STEPS = PASSES * QTILES
+LAST = STEPS - 1
 CHUNK = 256
 CS = CHUNK // PACK
 LINE = 4
-HEAD_V_SHARE = 40
+Q_LOADS = [(0, 1), (1, 2), (2, 4)]
+HEAD_VECTOR_S = 40
+EARLY_GATE = 8
+P_BUFS = 4
+W_BUFS = 3
+
+VECTOR_K_UNIT = 3
+SCALAR_K_UNITS = [7, 9]
+SCALAR_V_UNITS = [13, 15, 17, 19, 23, 25, 27, 27]
+QUANTIZE_Q_UNIT = 0
 
 
 def tile_rows_a_tanh_gate_kernel(tc, qT, kT, t, v, og, out):
     nc = tc.nc
     q_hbm = qT.rearrange("h (p j) n -> (h p) j n", j=PACK)
     k_hbm = kT.rearrange("h (p j) n -> (h p) j n", j=PACK)
-    v_hbm = v.rearrange("h (g p j) e -> g p h (j e)", p=P, j=PACK)
+    v_hbm = v.rearrange("h (g s r) e -> g s h (r e)", s=P, r=PACK)
+    t_hbm = t.rearrange("(g s r) o -> g s (r o)", s=P, r=PACK)
     og_hbm = og.rearrange("h (c q) e -> c q h e", q=QT)
     out_hbm = out.rearrange("h (c q) e -> c q h e", q=QT)
-    t_hbm = t.rearrange("(g p j) o -> g p (j o)", p=P, j=PACK)
 
     with ExitStack() as ctx:
         keep = ctx.enter_context(tc.tile_pool(name="keep", bufs=1))
-        ring = ctx.enter_context(tc.tile_pool(name="ring", bufs=3))
+        ring = ctx.enter_context(tc.tile_pool(name="ring", bufs=W_BUFS))
         psum = ctx.enter_context(tc.psum_pool(name="psum", bufs=1))
         ctx.enter_context(tc.manual_schedule())
 
-        def sb(name, shape, dtype):
+        def resident(name, shape, dtype):
             return keep.tile(shape, dtype, name=name, align_bytes=64)
 
-        t_sb = [sb("t_sb%d" % g, [P, PACK], F32) for g in range(PASSES)]
-        warm = sb("warm", [P, 8], F32)
-        warm_out = sb("warm_out", [P, 8], F32)
-        q_loads = [(0, 1), (1, 2), (2, 4)]
-        q_raw = [sb("q_raw%d" % c0, [P, PACK, (c1 - c0) * QT], F32) for c0, c1 in q_loads]
-        k_raw = [sb("k_raw%d" % c, [P, PACK, CHUNK], F32) for c in range(N // CHUNK)]
-        v_raw = [sb("v_raw%d" % g, [P, H, PACK * E], F32) for g in range(PASSES)]
-        og_raw = [sb("og_raw%d" % c, [P, H, E], F32) for c in range(QTILES)]
-        q_bf = sb("q_bf", [P, NQ, PACK], BF16)
-        k_bf = [sb("k_bf%d" % g, [P, PACK, P, PACK], BF16) for g in range(PASSES)]
-        v_bf = [sb("v_bf%d" % g, [P, H, E, PACK], BF16) for g in range(PASSES)]
-        q_codes = sb("q_codes", [P, NQ], U32)
-        q_scales = sb("q_scales", [P, NQ], U8)
-        k_codes = [sb("k_codes%d" % g, [P, PASS], U32) for g in range(PASSES)]
-        k_scales = [sb("k_scales%d" % g, [P, PASS], U8) for g in range(PASSES)]
-        v_codes = [sb("v_codes%d" % g, [P, H * E], U32) for g in range(PASSES)]
-        v_scales = [sb("v_scales%d" % g, [P, H * E], U8) for g in range(PASSES)]
-        w_codes = [sb("w_codes%d" % s, [P, H * QT], U32) for s in range(STEPS)]
-        w_scales = [sb("w_scales%d" % s, [P, H * QT], U8) for s in range(STEPS)]
-        gate = [sb("gate%d" % c, [P, H, E], F32) for c in range(QTILES)]
-        res = [sb("res%d" % c, [P, H, E], F32) for c in range(QTILES)]
+        t_sb = [resident("t_sb%d" % g, [P, PACK], F32) for g in range(PASSES)]
+        q_raw = [resident("q_raw%d" % c0, [P, PACK, (c1 - c0) * QT], F32) for c0, c1 in Q_LOADS]
+        k_raw = [resident("k_raw%d" % i, [P, PACK, CHUNK], F32) for i in range(N // CHUNK)]
+        v_raw = [resident("v_raw%d" % g, [P, H, PACK * E], F32) for g in range(PASSES)]
+        og_early = resident("og_early", [P, EARLY_GATE], F32)
+        og_raw = [resident("og_raw%d" % c, [P, H, E], F32) for c in range(QTILES)]
+        q_bf = resident("q_bf", [P, NQ, PACK], BF16)
+        k_bf = [resident("k_bf%d" % g, [P, PACK, P, PACK], BF16) for g in range(PASSES)]
+        v_bf = [resident("v_bf%d" % g, [P, H, E, PACK], BF16) for g in range(PASSES)]
+        q_codes = resident("q_codes", [P, NQ], U32)
+        q_scales = resident("q_scales", [P, NQ], U8)
+        k_codes = [resident("k_codes%d" % g, [P, PASS], U32) for g in range(PASSES)]
+        k_scales = [resident("k_scales%d" % g, [P, PASS], U8) for g in range(PASSES)]
+        v_codes = [resident("v_codes%d" % g, [P, H * E], U32) for g in range(PASSES)]
+        v_scales = [resident("v_scales%d" % g, [P, H * E], U8) for g in range(PASSES)]
+        w_codes = [resident("w_codes%d" % step, [P, H * QT], U32) for step in range(STEPS)]
+        w_scales = [resident("w_scales%d" % step, [P, H * QT], U8) for step in range(STEPS)]
+        gate = [resident("gate%d" % c, [P, H * E], F32) for c in range(QTILES)]
+        res = [resident("res%d" % c, [P, H, E], F32) for c in range(QTILES)]
         score_ps = [psum.tile([P, PACK, QT], F32, name="score_ps%d" % h) for h in range(H)]
         y_ps = [psum.tile([P, H, E], F32, name="y_ps%d" % c) for c in range(QTILES)]
         p_sb = {}
         w_bf = {}
 
-        def copy_on(engine, dst, src):
-            if engine == "vector":
-                nc.vector.tensor_copy(out=dst, in_=src)
-            else:
-                nc.scalar.copy(out=dst, in_=src)
+        def load_q(part):
+            c0, c1 = Q_LOADS[part]
+            nc.sync.dma_start(out=q_raw[part][:], in_=q_hbm[:, :, c0 * QT : c1 * QT])
+
+        def load_k(i):
+            nc.sync.dma_start(out=k_raw[i][:], in_=k_hbm[:, :, i * CHUNK : (i + 1) * CHUNK])
+
+        def vector_copy(dst, src):
+            nc.vector.tensor_copy(out=dst, in_=src)
+
+        def scalar_copy(dst, src):
+            nc.scalar.copy(out=dst, in_=src)
 
         def quantize(codes, scales, src):
             nc.vector.quantize_mx(out=codes.bitcast(FP8X4), scales=scales, in_=src)
 
-        def load_q(part):
-            c0, c1 = q_loads[part]
-            nc.sync.dma_start(out=q_raw[part][:], in_=q_hbm[:, :, c0 * QT : c1 * QT])
-
-        def cast_q(engine, part):
-            c0, c1 = q_loads[part]
-            copy_on(
-                engine,
-                q_bf[:, c0 * QT : c1 * QT, :].rearrange("p (c i) j -> p c j i", i=LINE),
-                q_raw[part][:].rearrange("p j (c i) -> p c j i", i=LINE),
+        def round_q(copy, part):
+            c0, c1 = Q_LOADS[part]
+            copy(
+                q_bf[:, c0 * QT : c1 * QT, :].rearrange("p (n i) j -> p n j i", i=LINE),
+                q_raw[part][:].rearrange("p j (n i) -> p n j i", i=LINE),
             )
 
-        def quantize_q(c0, c1):
+        def quantize_q(part):
+            c0, c1 = Q_LOADS[part]
             cols = slice(c0 * QT, c1 * QT)
             quantize(q_codes[:, cols], q_scales[:, cols], q_bf[:, cols, :].rearrange("p n j -> p (n j)"))
 
-        def cast_k(engine, c, s0, s1):
-            g, first = divmod(c * CS, P)
-            copy_on(
-                engine,
+        def round_k(copy, i, s0, s1):
+            g, first = divmod(i * CS, P)
+            copy(
                 k_bf[g][:, :, first + s0 : first + s1, :].rearrange("p r s j -> p s j r"),
-                k_raw[c][:, :, s0 * PACK : s1 * PACK].rearrange("p j (s r) -> p s j r", r=PACK),
+                k_raw[i][:, :, s0 * PACK : s1 * PACK].rearrange("p j (s r) -> p s j r", r=PACK),
             )
 
-        def quantize_k_part(c, r):
-            g, first = divmod(c * CS, P)
+        def quantize_k_part(i, r):
+            g, first = divmod(i * CS, P)
             cols = slice(r * P + first, r * P + first + CS)
-            quantize(
-                k_codes[g][:, cols],
-                k_scales[g][:, cols],
-                k_bf[g][:, r, first : first + CS, :].rearrange("p s j -> p (s j)"),
-            )
+            src = k_bf[g][:, r, first : first + CS, :].rearrange("p s j -> p (s j)")
+            quantize(k_codes[g][:, cols], k_scales[g][:, cols], src)
 
         def quantize_k(g):
             quantize(k_codes[g][:], k_scales[g][:], k_bf[g][:].rearrange("p r s j -> p (r s j)"))
 
-        def cast_v(engine, g, h):
-            copy_on(
-                engine,
-                v_bf[g][:, h, :, :].rearrange("p (c i) j -> p c j i", i=LINE),
-                v_raw[g][:, h, :].rearrange("p (j c i) -> p c j i", j=PACK, i=LINE),
+        def round_v(g, h):
+            scalar_copy(
+                v_bf[g][:, h, :, :].rearrange("s (n i) r -> s n r i", i=LINE),
+                v_raw[g][:, h, :].rearrange("s (r n i) -> s n r i", r=PACK, i=LINE),
             )
 
         def quantize_v(g):
-            quantize(v_codes[g][:], v_scales[g][:], v_bf[g][:].rearrange("p h e j -> p (h e j)"))
+            quantize(v_codes[g][:], v_scales[g][:], v_bf[g][:].rearrange("s h e r -> s (h e r)"))
 
-        def score(s, h, r):
-            g, c = divmod(s, QTILES)
+        def score(step, h, r):
+            g, c = divmod(step, QTILES)
             rows = slice(h * ROWS, (h + 1) * ROWS)
-            tok = slice(r * P, (r + 1) * P)
-            qs = slice(c * QT, (c + 1) * QT)
+            tokens = slice(r * P, (r + 1) * P)
+            queries = slice(c * QT, (c + 1) * QT)
             nc.tensor.matmul_mx(
                 out=score_ps[h][:, r, :],
-                lhsT=k_codes[g][rows, tok].bitcast(FP8X4),
-                lhsT_scale=k_scales[g][rows, tok],
-                rhs=q_codes[rows, qs].bitcast(FP8X4),
-                rhs_scale=q_scales[rows, qs],
+                lhsT=k_codes[g][rows, tokens].bitcast(FP8X4),
+                lhsT_scale=k_scales[g][rows, tokens],
+                rhs=q_codes[rows, queries].bitcast(FP8X4),
+                rhs_scale=q_scales[rows, queries],
                 start=True,
                 stop=True,
             )
 
-        def tanh(s, h):
+        def tanh(step, h):
             if h == 0:
-                p_sb[s] = ring.tile([P, H, QT, PACK], F32, name="p_sb", bufs=4)
+                p_sb[step] = ring.tile([P, H, QT, PACK], F32, name="p_sb", bufs=P_BUFS)
             nc.scalar.activation(
-                out=p_sb[s][:, h, :, :], in_=score_ps[h][:].rearrange("p r q -> p q r"), func=ACT.Tanh
+                out=p_sb[step][:, h, :, :], in_=score_ps[h][:].rearrange("s r q -> s q r"), func=ACT.Tanh
             )
-            if s + 1 < STEPS:
+            if step < LAST:
                 for r in range(PACK):
-                    score(s + 1, h, r)
+                    score(step + 1, h, r)
 
-        def weigh(s, h0, h1):
+        def weigh(step, h0, h1):
             if h0 == 0:
-                w_bf[s] = ring.tile([P, H, QT, PACK], BF16, name="w_bf", align_bytes=64)
-            n = (h1 - h0) * QT
+                w_bf[step] = ring.tile([P, H, QT, PACK], BF16, name="w_bf", align_bytes=64)
             nc.vector.tensor_tensor(
-                out=w_bf[s][:, h0:h1, :, :].rearrange("p h q r -> p (h q) r"),
-                in0=p_sb[s][:, h0:h1, :, :].rearrange("p h q r -> p (h q) r"),
-                in1=t_sb[s // QTILES][:].unsqueeze(1).to_broadcast([P, n, PACK]),
+                out=w_bf[step][:, h0:h1, :, :].rearrange("s h q r -> s (h q) r"),
+                in0=p_sb[step][:, h0:h1, :, :].rearrange("s h q r -> s (h q) r"),
+                in1=t_sb[step // QTILES][:].unsqueeze(1).to_broadcast([P, (h1 - h0) * QT, PACK]),
                 op=ALU.mult,
             )
 
-        def quantize_w(s, h0, h1):
+        def quantize_w(step, h0, h1):
             cols = slice(h0 * QT, h1 * QT)
-            quantize(
-                w_codes[s][:, cols], w_scales[s][:, cols], w_bf[s][:, h0:h1, :, :].rearrange("p h q r -> p (h q r)")
-            )
+            src = w_bf[step][:, h0:h1, :, :].rearrange("s h q r -> s (h q r)")
+            quantize(w_codes[step][:, cols], w_scales[step][:, cols], src)
 
         def y_bank(c, h):
-            return y_ps[0] if (c == QTILES - 1 and h >= 2) else y_ps[c]
+            return y_ps[0] if (c == QTILES - 1 and h >= H // 2) else y_ps[c]
 
-        def mix(c, h0, h1, passes=range(PASSES)):
+        def mix(c, h0, h1):
             for h in range(h0, h1):
                 cols = slice(h * QT, (h + 1) * QT)
-                for g in passes:
-                    s = g * QTILES + c
+                for g in range(PASSES):
+                    step = g * QTILES + c
                     nc.tensor.matmul_mx(
                         out=y_bank(c, h)[:, h, :],
-                        lhsT=w_codes[s][:, cols].bitcast(FP8X4),
-                        lhsT_scale=w_scales[s][:, cols],
+                        lhsT=w_codes[step][:, cols].bitcast(FP8X4),
+                        lhsT_scale=w_scales[step][:, cols],
                         rhs=v_codes[g][:, cols].bitcast(FP8X4),
                         rhs_scale=v_scales[g][:, cols],
                         start=(g == 0),
@@ -187,27 +191,30 @@ def tile_rows_a_tanh_gate_kernel(tc, qT, kT, t, v, og, out):
                     )
 
         def sigmoid(c):
-            nc.scalar.activation(out=gate[c][:], in_=og_raw[c][:], func=ACT.Sigmoid)
+            first = EARLY_GATE if c == 0 else 0
+            src = og_raw[c][:].rearrange("q h e -> q (h e)")
+            nc.scalar.activation(out=gate[c][:, first:], in_=src[:, first:], func=ACT.Sigmoid)
 
         def finish(c, h0, h1, queue):
             nc.vector.scalar_tensor_tensor(
-                out=res[c][:, h0:h1, :].rearrange("p h e -> p (h e)"),
-                in0=y_bank(c, h0)[:, h0:h1, :].rearrange("p h e -> p (h e)"),
+                out=res[c][:, h0:h1, :].rearrange("q h e -> q (h e)"),
+                in0=y_bank(c, h0)[:, h0:h1, :].rearrange("q h e -> q (h e)"),
                 scalar=1.0 / 16.0,
-                in1=gate[c][:, h0:h1, :].rearrange("p h e -> p (h e)"),
+                in1=gate[c][:, h0 * E : h1 * E],
                 op0=ALU.mult,
                 op1=ALU.mult,
             )
             queue.dma_start(out=out_hbm[c][:, h0:h1, :], in_=res[c][:, h0:h1, :])
 
+        nc.scalar.dma_start(out=og_early[:], in_=og_hbm[0][:, 0, 0:EARLY_GATE])
         load_q(0)
-        for c in range(2):
-            nc.sync.dma_start(out=k_raw[c][:], in_=k_hbm[:, :, c * CHUNK : (c + 1) * CHUNK])
+        load_k(0)
+        load_k(1)
         load_q(1)
         load_q(2)
         nc.sync.dma_start(out=t_sb[0][:], in_=t_hbm[0])
-        for c in range(2, 4):
-            nc.sync.dma_start(out=k_raw[c][:], in_=k_hbm[:, :, c * CHUNK : (c + 1) * CHUNK])
+        load_k(2)
+        load_k(3)
         nc.sync.dma_start(out=t_sb[1][:], in_=t_hbm[1])
         for g in range(PASSES):
             for h0 in range(0, H, 2):
@@ -215,81 +222,76 @@ def tile_rows_a_tanh_gate_kernel(tc, qT, kT, t, v, og, out):
         for c in range(QTILES):
             nc.sync.dma_start(out=og_raw[c][:], in_=og_hbm[c])
 
-        nc.vector.memset(warm[:], 0.0)
-        nc.scalar.activation(out=warm_out[:], in_=warm[:], func=ACT.Sigmoid)
+        nc.scalar.activation(out=gate[0][:, 0:EARLY_GATE], in_=og_early[:], func=ACT.Sigmoid)
 
-        cast_q("vector", 0)
-        cast_k("scalar", 0, HEAD_V_SHARE, CS)
-        cast_k("vector", 0, 0, HEAD_V_SHARE)
-        quantize_q(0, 1)
-        quantize_k_part(0, 0)
-        quantize_k_part(0, 1)
-        cast_k("scalar", 1, HEAD_V_SHARE, CS)
-        cast_k("vector", 1, 0, HEAD_V_SHARE)
-        quantize_k_part(0, 2)
-        quantize_k_part(0, 3)
+        round_q(vector_copy, 0)
+        round_k(scalar_copy, 0, HEAD_VECTOR_S, CS)
+        round_k(vector_copy, 0, 0, HEAD_VECTOR_S)
+        quantize_q(0)
+        for r in range(PACK - 1):
+            quantize_k_part(0, r)
+        round_k(scalar_copy, 1, HEAD_VECTOR_S, CS)
+        round_k(vector_copy, 1, 0, HEAD_VECTOR_S)
+        quantize_k_part(0, PACK - 1)
         for r in range(PACK):
             quantize_k_part(1, r)
-            for h in range(H):
+            score(0, 0, r)
+        for h in range(1, H):
+            for r in range(PACK):
                 score(0, h, r)
-        cast_q("scalar", 1)
-        quantize_q(1, 2)
-        cast_q("vector", 2)
+        round_q(scalar_copy, 1)
+        quantize_q(1)
+        round_q(vector_copy, 2)
 
-        scalar_v_slots = [11, 15, 19, 21, 23, 25]
-        after_tanh = {}
-        for i, u in enumerate(scalar_v_slots):
-            after_tanh[u] = [lambda i=i: cast_v("scalar", *divmod(i + 2, H))]
-        after_tanh[27] = [lambda: mix(0, 0, H)]
-        after_weigh = {
-            0: lambda: quantize_q(2, 4),
-            2: lambda: cast_k("vector", 2, 0, CS),
-            5: lambda: cast_k("vector", 3, 0, CS),
-            7: lambda: quantize_k(1),
-            11: lambda: cast_v("vector", 0, 0),
-            13: lambda: cast_v("vector", 0, 1),
-            19: lambda: quantize_v(0),
-            25: lambda: quantize_v(1),
-        }
-
-        last = STEPS - 1
-        for s in range(last):
+        for step in range(LAST):
             for h in range(H):
-                u = s * H + h
-                tanh(s, h)
-                for job in after_tanh.get(u, []):
-                    job()
-                if s == 0:
-                    weigh(s, h, h + 1)
+                unit = step * H + h
+                tanh(step, h)
+                if unit in SCALAR_K_UNITS:
+                    s0 = SCALAR_K_UNITS.index(unit) * (CS // 2)
+                    round_k(scalar_copy, 3, s0, s0 + CS // 2)
+                for i, v_unit in enumerate(SCALAR_V_UNITS):
+                    if v_unit == unit:
+                        round_v(*divmod(i, H))
+                if step == 0:
+                    weigh(step, h, h + 1)
                 elif h % 2 == 1:
-                    weigh(s, h - 1, h + 1)
-                if s > 0 and h == 1:
-                    quantize_w(s - 1, 0, H)
-                if u in after_weigh:
-                    after_weigh[u]()
+                    weigh(step, h - 1, h + 1)
+                if step > 0 and h == 1:
+                    quantize_w(step - 1, 0, H)
+                if unit == QUANTIZE_Q_UNIT:
+                    quantize_q(2)
+                if unit == VECTOR_K_UNIT:
+                    round_k(vector_copy, 2, 0, CS)
+                if unit == SCALAR_K_UNITS[-1]:
+                    quantize_k(1)
+                for g in range(PASSES):
+                    if unit == SCALAR_V_UNITS[(g + 1) * H - 1]:
+                        quantize_v(g)
 
-        tanh(last, 0)
-        mix(1, 0, H)
-        tanh(last, 1)
+        c_last = QTILES - 1
+        quantize_w(LAST - 1, 0, H)
+        for c in range(c_last):
+            mix(c, 0, H)
+        tanh(LAST, 0)
+        tanh(LAST, 1)
         sigmoid(0)
+        tanh(LAST, 2)
         sigmoid(1)
-        weigh(last, 0, 2)
-        quantize_w(last - 1, 0, H)
-        mix(2, 0, H)
-        finish(0, 0, H, nc.sync)
-        tanh(last, 2)
+        tanh(LAST, 3)
         sigmoid(2)
-        weigh(last, 2, 3)
-        quantize_w(last, 0, 2)
-        mix(3, 0, 2)
-        finish(1, 0, H, nc.sync)
-        finish(2, 0, H, nc.sync)
-        tanh(last, 3)
         sigmoid(3)
-        weigh(last, 3, 4)
-        quantize_w(last, 2, 3)
-        mix(3, 2, 3)
-        quantize_w(last, 3, 4)
-        mix(3, 3, 4)
-        finish(3, 0, 2, nc.sync)
-        finish(3, 2, 4, nc.scalar)
+        weigh(LAST, 0, 2)
+        weigh(LAST, 2, 3)
+        finish(0, 0, H, nc.sync)
+        quantize_w(LAST, 0, 2)
+        mix(c_last, 0, 2)
+        finish(1, 0, H, nc.sync)
+        weigh(LAST, 3, 4)
+        quantize_w(LAST, 2, 3)
+        mix(c_last, 2, 3)
+        finish(2, 0, H, nc.sync)
+        quantize_w(LAST, 3, 4)
+        mix(c_last, 3, 4)
+        finish(c_last, 0, 2, nc.sync)
+        finish(c_last, 2, 4, nc.scalar)

from contextlib import ExitStack

import concourse.mybir as mybir

H, D, NQ, N, E = 4, 128, 512, 1024, 128
FLOPS = 2 * H * N * NQ * (D + E)

F32 = mybir.dt.float32
BF16 = mybir.dt.bfloat16
U32 = mybir.dt.uint32
U8 = mybir.dt.uint8
FP8X4 = mybir.dt.float8_e4m3fn_x4
ACT = mybir.ActivationFunctionType
ALU = mybir.AluOpType

P = 128
PACK = 4
ROWS = D // PACK
PASS = P * PACK
PASSES = N // PASS
QT = 128
QTILES = NQ // QT
STEPS = PASSES * QTILES
LAST = STEPS - 1
CHUNK = 256
CS = CHUNK // PACK
LINE = 4
Q_LOADS = [(0, 1), (1, 2), (2, 4)]
HEAD_VECTOR_S = 40
EARLY_GATE = 8
P_BUFS = 4
W_BUFS = 3

VECTOR_K_UNIT = 3
SCALAR_K_UNITS = [7, 9]
SCALAR_V_UNITS = [13, 15, 17, 19, 23, 25, 27, 27]
QUANTIZE_Q_UNIT = 0


def tile_rows_a_tanh_gate_kernel(tc, qT, kT, t, v, og, out):
    nc = tc.nc
    q_hbm = qT.rearrange("h (p j) n -> (h p) j n", j=PACK)
    k_hbm = kT.rearrange("h (p j) n -> (h p) j n", j=PACK)
    v_hbm = v.rearrange("h (g s r) e -> g s h (r e)", s=P, r=PACK)
    t_hbm = t.rearrange("(g s r) o -> g s (r o)", s=P, r=PACK)
    og_hbm = og.rearrange("h (c q) e -> c q h e", q=QT)
    out_hbm = out.rearrange("h (c q) e -> c q h e", q=QT)

    with ExitStack() as ctx:
        keep = ctx.enter_context(tc.tile_pool(name="keep", bufs=1))
        ring = ctx.enter_context(tc.tile_pool(name="ring", bufs=W_BUFS))
        psum = ctx.enter_context(tc.psum_pool(name="psum", bufs=1))
        ctx.enter_context(tc.manual_schedule())

        def resident(name, shape, dtype):
            return keep.tile(shape, dtype, name=name, align_bytes=64)

        t_sb = [resident("t_sb%d" % g, [P, PACK], F32) for g in range(PASSES)]
        q_raw = [resident("q_raw%d" % c0, [P, PACK, (c1 - c0) * QT], F32) for c0, c1 in Q_LOADS]
        k_raw = [resident("k_raw%d" % i, [P, PACK, CHUNK], F32) for i in range(N // CHUNK)]
        v_raw = [resident("v_raw%d" % g, [P, H, PACK * E], F32) for g in range(PASSES)]
        og_early = resident("og_early", [P, EARLY_GATE], F32)
        og_raw = [resident("og_raw%d" % c, [P, H, E], F32) for c in range(QTILES)]
        q_bf = resident("q_bf", [P, NQ, PACK], BF16)
        k_bf = [resident("k_bf%d" % g, [P, PACK, P, PACK], BF16) for g in range(PASSES)]
        v_bf = [resident("v_bf%d" % g, [P, H, E, PACK], BF16) for g in range(PASSES)]
        q_codes = resident("q_codes", [P, NQ], U32)
        q_scales = resident("q_scales", [P, NQ], U8)
        k_codes = [resident("k_codes%d" % g, [P, PASS], U32) for g in range(PASSES)]
        k_scales = [resident("k_scales%d" % g, [P, PASS], U8) for g in range(PASSES)]
        v_codes = [resident("v_codes%d" % g, [P, H * E], U32) for g in range(PASSES)]
        v_scales = [resident("v_scales%d" % g, [P, H * E], U8) for g in range(PASSES)]
        w_codes = [resident("w_codes%d" % step, [P, H * QT], U32) for step in range(STEPS)]
        w_scales = [resident("w_scales%d" % step, [P, H * QT], U8) for step in range(STEPS)]
        gate = [resident("gate%d" % c, [P, H * E], F32) for c in range(QTILES)]
        res = [resident("res%d" % c, [P, H, E], F32) for c in range(QTILES)]
        score_ps = [psum.tile([P, PACK, QT], F32, name="score_ps%d" % h) for h in range(H)]
        y_ps = [psum.tile([P, H, E], F32, name="y_ps%d" % c) for c in range(QTILES)]
        p_sb = {}
        w_bf = {}

        def load_q(part):
            c0, c1 = Q_LOADS[part]
            nc.sync.dma_start(out=q_raw[part][:], in_=q_hbm[:, :, c0 * QT : c1 * QT])

        def load_k(i):
            nc.sync.dma_start(out=k_raw[i][:], in_=k_hbm[:, :, i * CHUNK : (i + 1) * CHUNK])

        def vector_copy(dst, src):
            nc.vector.tensor_copy(out=dst, in_=src)

        def scalar_copy(dst, src):
            nc.scalar.copy(out=dst, in_=src)

        def quantize(codes, scales, src):
            nc.vector.quantize_mx(out=codes.bitcast(FP8X4), scales=scales, in_=src)

        def round_q(copy, part):
            c0, c1 = Q_LOADS[part]
            copy(
                q_bf[:, c0 * QT : c1 * QT, :].rearrange("p (n i) j -> p n j i", i=LINE),
                q_raw[part][:].rearrange("p j (n i) -> p n j i", i=LINE),
            )

        def quantize_q(part):
            c0, c1 = Q_LOADS[part]
            cols = slice(c0 * QT, c1 * QT)
            quantize(q_codes[:, cols], q_scales[:, cols], q_bf[:, cols, :].rearrange("p n j -> p (n j)"))

        def round_k(copy, i, s0, s1):
            g, first = divmod(i * CS, P)
            copy(
                k_bf[g][:, :, first + s0 : first + s1, :].rearrange("p r s j -> p s j r"),
                k_raw[i][:, :, s0 * PACK : s1 * PACK].rearrange("p j (s r) -> p s j r", r=PACK),
            )

        def quantize_k_part(i, r):
            g, first = divmod(i * CS, P)
            cols = slice(r * P + first, r * P + first + CS)
            src = k_bf[g][:, r, first : first + CS, :].rearrange("p s j -> p (s j)")
            quantize(k_codes[g][:, cols], k_scales[g][:, cols], src)

        def quantize_k(g):
            quantize(k_codes[g][:], k_scales[g][:], k_bf[g][:].rearrange("p r s j -> p (r s j)"))

        def round_v(g, h):
            scalar_copy(
                v_bf[g][:, h, :, :].rearrange("s (n i) r -> s n r i", i=LINE),
                v_raw[g][:, h, :].rearrange("s (r n i) -> s n r i", r=PACK, i=LINE),
            )

        def quantize_v(g):
            quantize(v_codes[g][:], v_scales[g][:], v_bf[g][:].rearrange("s h e r -> s (h e r)"))

        def score(step, h, r):
            g, c = divmod(step, QTILES)
            rows = slice(h * ROWS, (h + 1) * ROWS)
            tokens = slice(r * P, (r + 1) * P)
            queries = slice(c * QT, (c + 1) * QT)
            nc.tensor.matmul_mx(
                out=score_ps[h][:, r, :],
                lhsT=k_codes[g][rows, tokens].bitcast(FP8X4),
                lhsT_scale=k_scales[g][rows, tokens],
                rhs=q_codes[rows, queries].bitcast(FP8X4),
                rhs_scale=q_scales[rows, queries],
                start=True,
                stop=True,
            )

        def tanh(step, h):
            if h == 0:
                p_sb[step] = ring.tile([P, H, QT, PACK], F32, name="p_sb", bufs=P_BUFS)
            nc.scalar.activation(
                out=p_sb[step][:, h, :, :], in_=score_ps[h][:].rearrange("s r q -> s q r"), func=ACT.Tanh
            )
            if step < LAST:
                for r in range(PACK):
                    score(step + 1, h, r)

        def weigh(step, h0, h1):
            if h0 == 0:
                w_bf[step] = ring.tile([P, H, QT, PACK], BF16, name="w_bf", align_bytes=64)
            nc.vector.tensor_tensor(
                out=w_bf[step][:, h0:h1, :, :].rearrange("s h q r -> s (h q) r"),
                in0=p_sb[step][:, h0:h1, :, :].rearrange("s h q r -> s (h q) r"),
                in1=t_sb[step // QTILES][:].unsqueeze(1).to_broadcast([P, (h1 - h0) * QT, PACK]),
                op=ALU.mult,
            )

        def quantize_w(step, h0, h1):
            cols = slice(h0 * QT, h1 * QT)
            src = w_bf[step][:, h0:h1, :, :].rearrange("s h q r -> s (h q r)")
            quantize(w_codes[step][:, cols], w_scales[step][:, cols], src)

        def y_bank(c, h):
            return y_ps[0] if (c == QTILES - 1 and h >= H // 2) else y_ps[c]

        def mix(c, h0, h1):
            for h in range(h0, h1):
                cols = slice(h * QT, (h + 1) * QT)
                for g in range(PASSES):
                    step = g * QTILES + c
                    nc.tensor.matmul_mx(
                        out=y_bank(c, h)[:, h, :],
                        lhsT=w_codes[step][:, cols].bitcast(FP8X4),
                        lhsT_scale=w_scales[step][:, cols],
                        rhs=v_codes[g][:, cols].bitcast(FP8X4),
                        rhs_scale=v_scales[g][:, cols],
                        start=(g == 0),
                        stop=(g == PASSES - 1),
                    )

        def sigmoid(c):
            first = EARLY_GATE if c == 0 else 0
            src = og_raw[c][:].rearrange("q h e -> q (h e)")
            nc.scalar.activation(out=gate[c][:, first:], in_=src[:, first:], func=ACT.Sigmoid)

        def finish(c, h0, h1, queue):
            nc.vector.scalar_tensor_tensor(
                out=res[c][:, h0:h1, :].rearrange("q h e -> q (h e)"),
                in0=y_bank(c, h0)[:, h0:h1, :].rearrange("q h e -> q (h e)"),
                scalar=1.0 / 16.0,
                in1=gate[c][:, h0 * E : h1 * E],
                op0=ALU.mult,
                op1=ALU.mult,
            )
            queue.dma_start(out=out_hbm[c][:, h0:h1, :], in_=res[c][:, h0:h1, :])

        nc.scalar.dma_start(out=og_early[:], in_=og_hbm[0][:, 0, 0:EARLY_GATE])
        load_q(0)
        load_k(0)
        load_k(1)
        load_q(1)
        load_q(2)
        nc.sync.dma_start(out=t_sb[0][:], in_=t_hbm[0])
        load_k(2)
        load_k(3)
        nc.sync.dma_start(out=t_sb[1][:], in_=t_hbm[1])
        for g in range(PASSES):
            for h0 in range(0, H, 2):
                nc.sync.dma_start(out=v_raw[g][:, h0 : h0 + 2, :], in_=v_hbm[g][:, h0 : h0 + 2, :])
        for c in range(QTILES):
            nc.sync.dma_start(out=og_raw[c][:], in_=og_hbm[c])

        nc.scalar.activation(out=gate[0][:, 0:EARLY_GATE], in_=og_early[:], func=ACT.Sigmoid)

        round_q(vector_copy, 0)
        round_k(scalar_copy, 0, HEAD_VECTOR_S, CS)
        round_k(vector_copy, 0, 0, HEAD_VECTOR_S)
        quantize_q(0)
        for r in range(PACK - 1):
            quantize_k_part(0, r)
        round_k(scalar_copy, 1, HEAD_VECTOR_S, CS)
        round_k(vector_copy, 1, 0, HEAD_VECTOR_S)
        quantize_k_part(0, PACK - 1)
        for r in range(PACK):
            quantize_k_part(1, r)
            score(0, 0, r)
        for h in range(1, H):
            for r in range(PACK):
                score(0, h, r)
        round_q(scalar_copy, 1)
        quantize_q(1)
        round_q(vector_copy, 2)

        for step in range(LAST):
            for h in range(H):
                unit = step * H + h
                tanh(step, h)
                if unit in SCALAR_K_UNITS:
                    s0 = SCALAR_K_UNITS.index(unit) * (CS // 2)
                    round_k(scalar_copy, 3, s0, s0 + CS // 2)
                for i, v_unit in enumerate(SCALAR_V_UNITS):
                    if v_unit == unit:
                        round_v(*divmod(i, H))
                if step == 0:
                    weigh(step, h, h + 1)
                elif h % 2 == 1:
                    weigh(step, h - 1, h + 1)
                if step > 0 and h == 1:
                    quantize_w(step - 1, 0, H)
                if unit == QUANTIZE_Q_UNIT:
                    quantize_q(2)
                if unit == VECTOR_K_UNIT:
                    round_k(vector_copy, 2, 0, CS)
                if unit == SCALAR_K_UNITS[-1]:
                    quantize_k(1)
                for g in range(PASSES):
                    if unit == SCALAR_V_UNITS[(g + 1) * H - 1]:
                        quantize_v(g)

        c_last = QTILES - 1
        quantize_w(LAST - 1, 0, H)
        for c in range(c_last):
            mix(c, 0, H)
        tanh(LAST, 0)
        tanh(LAST, 1)
        sigmoid(0)
        tanh(LAST, 2)
        sigmoid(1)
        tanh(LAST, 3)
        sigmoid(2)
        sigmoid(3)
        weigh(LAST, 0, 2)
        weigh(LAST, 2, 3)
        finish(0, 0, H, nc.sync)
        quantize_w(LAST, 0, 2)
        mix(c_last, 0, 2)
        finish(1, 0, H, nc.sync)
        weigh(LAST, 3, 4)
        quantize_w(LAST, 2, 3)
        mix(c_last, 2, 3)
        finish(2, 0, H, nc.sync)
        quantize_w(LAST, 3, 4)
        mix(c_last, 3, 4)
        finish(c_last, 0, 2, nc.sync)
        finish(c_last, 2, 4, nc.scalar)
